import numpy as np
import ml_dtypes


def mxq(x, axis, fmt="e4m3"):
    dtype, down = {"e4m3": (ml_dtypes.float8_e4m3fn, 7), "e5m2": (ml_dtypes.float8_e5m2, 14)}[fmt]
    v = np.moveaxis(np.asarray(x, np.float32).astype(ml_dtypes.bfloat16).astype(np.float64), axis, -1)
    blocks = v.reshape(v.shape[:-1] + (-1, 32))
    amax = np.abs(blocks).max(-1, keepdims=True)
    byte = np.maximum(np.where(amax > 0, np.frexp(amax)[1] - 1 + 127, 0) - down, 1)
    scale = np.exp2(byte - 127.0)
    codes = (blocks / scale).astype(np.float32).astype(dtype).astype(np.float64)
    return np.moveaxis((codes * scale).reshape(v.shape), -1, axis)


WIDE = False


def mx_kscale(k):
    if not WIDE:
        return np.ones(k)
    levels = np.array([10, -10, 5, -5, 0])
    if k % 512:
        return np.exp2(np.random.permutation(np.resize(levels, k // 32))).repeat(32)
    a = np.empty((k // 512, 16))
    for p in range(k // 512):
        a[p, :8] = np.random.permutation(np.resize(levels, 8))
        for g in range(8):
            far = levels[np.abs(levels - a[p, g]) >= 10]
            a[p, g + 8] = far[np.random.randint(len(far))]
    return np.exp2(a.ravel()).repeat(32)


def f64(x):
    return np.asarray(x).astype(np.float64)


def striped(idx):
    return np.tile(idx.reshape(-1, 16).T, (8, 1)).astype(np.uint16)


def unstriped(offs):
    return offs[:16].T.reshape(-1).astype(np.int64)


def pack_weight(w):
    k, n = w.shape
    w = f64(np.asarray(w, np.float32).astype(ml_dtypes.bfloat16)).reshape(k // 32, 32, n)
    amax = np.abs(w).max(1)
    byte = np.clip(np.where(amax > 0, np.frexp(amax)[1] - 1 + 127 - 7, 1), 1, 254)
    scaled = (w * np.exp2(127.0 - byte)[:, None, :]).reshape(k, n).astype(np.float32)
    words = np.ascontiguousarray(scaled.reshape(k // 512, 128, 4, n).transpose(0, 1, 3, 2)).astype(ml_dtypes.float8_e4m3fn).view(np.uint8)
    return words, np.ascontiguousarray(byte.astype(np.uint8).reshape(k // 512, 16, n))


def unpack_weight(words, scales):
    g, p, n, _ = words.shape
    vals = np.ascontiguousarray(words).view(ml_dtypes.float8_e4m3fn).astype(np.float64) * np.repeat(np.exp2(scales.astype(np.float64) - 127.0), 8, axis=1)[..., None]
    return vals.transpose(0, 1, 3, 2).reshape(g * 512, n)


E2M1 = np.array([0.0, 0.5, 1.0, 1.5, 2.0, 3.0, 4.0, 6.0, -0.0, -0.5, -1.0, -1.5, -2.0, -3.0, -4.0, -6.0])


def pack_fp4(w):
    k, n = w.shape
    w = f64(np.asarray(w, np.float32).astype(ml_dtypes.bfloat16)).reshape(k // 32, 32, n)
    amax = np.abs(w).max(1)
    mant, ex = np.frexp(amax / 6.0)
    byte = np.clip(np.where(amax > 0, np.where(mant > 0.5, ex, ex - 1) + 127, 1), 1, 254)
    scaled = (w * np.exp2(127.0 - byte)[:, None, :]).reshape(k, n).astype(np.float32)
    c = np.ascontiguousarray(scaled.reshape(k // 512, 128, 4, n).transpose(0, 1, 3, 2)).astype(ml_dtypes.float4_e2m1fn).view(np.uint8) & 0xF
    words = (c[..., 0::2] | (c[..., 1::2] << 4)).reshape(k // 512, 128, 2 * n)
    return np.ascontiguousarray(words), np.ascontiguousarray(byte.astype(np.uint8).reshape(k // 512, 16, n))


def unpack_fp4(words, scales):
    g, _, n = scales.shape
    words = np.ascontiguousarray(words).reshape(g, 128, n, 2)
    nib = np.empty((g, 128, n, 4), np.uint8)
    nib[..., 0::2] = words & 0xF
    nib[..., 1::2] = words >> 4
    vals = E2M1[nib] * np.repeat(np.exp2(scales.astype(np.float64) - 127.0), 8, axis=1)[..., None]
    return vals.transpose(0, 1, 3, 2).reshape(g * 512, n)


def sigmoid(v):
    return 1.0 / (1.0 + np.exp(-np.maximum(v, -700.0)))


K, T, S, D, N, H = 512, 4096, 1024, 4, 256, 512


def setup_inputs():
    n = np.random.standard_normal
    s = mx_kscale(K)[:, None]
    u = mx_kscale(H)
    packed_xT = pack_weight(n((K, T)) * s)
    packed_w1 = pack_fp4(n((K, H)) / np.sqrt(K) / s)
    packed_w2 = pack_fp4(n((K, H)) / np.sqrt(K) / s)
    packed_w3 = pack_fp4(n((H, N)) / np.sqrt(H) / u[:, None])
    return {
        "x_words": packed_xT[0],
        "x_scales": packed_xT[1],
        "w1_words": packed_w1[0],
        "w1_scales": packed_w1[1],
        "w2_words": packed_w2[0],
        "w2_scales": packed_w2[1],
        "unit": (np.random.uniform(0.6, 1.4, (H, 1)) * u[:, None]).astype(np.float32),
        "w3_words": packed_w3[0],
        "w3_scales": packed_w3[1],
        "offs": striped(np.random.permutation(T)[:S]),
        "pf": striped(np.random.permutation(S)),
    }


def reference(x_words, x_scales, w1_words, w1_scales, w2_words, w2_scales, unit, w3_words, w3_scales, offs, pf):
    xq = unpack_weight(x_words, x_scales)[:, unstriped(offs)]
    fr = unpack_fp4(w2_words, w2_scales).T @ xq
    freq = np.log(np.exp(fr) + 1.0)
    rc = unpack_fp4(w1_words, w1_scales).T @ xq
    recy = np.log(np.exp(rc) + 1.0)
    util = freq / (recy + 0.4)
    vict = util.reshape(len(util), -1, D).min(axis=2)
    marg = util - np.repeat(vict, D, axis=1)
    upf = util[:, unstriped(pf)]
    adm = sigmoid(1.5 * (upf - util))
    hid = f64(unit) * (marg - (0.4 * np.log(adm + 0.1)))
    return unpack_fp4(w3_words, w3_scales).T @ mxq(hid, 0, "e4m3")

@@ -1,0 +1,209 @@
+from contextlib import ExitStack
+
+import concourse.mybir as mybir
+
+K, T, S, D, N, H = 512, 4096, 1024, 4, 256, 512
+FLOPS = 2 * K * H * S * 2 + 2 * H * N * S
+
+F32 = mybir.dt.float32
+BF16 = mybir.dt.bfloat16
+I32 = mybir.dt.int32
+U32 = mybir.dt.uint32
+U16 = mybir.dt.uint16
+U8 = mybir.dt.uint8
+FP8X4 = mybir.dt.float8_e4m3fn_x4
+FP4X4 = mybir.dt.float4_e2m1fn_x4
+ACT = mybir.ActivationFunctionType
+ALU = mybir.AluOpType
+
+P = 128
+PACK = 4
+HALF = 512
+LN_BLOCKS = 8
+OUT_COLS = 256
+LINEAR_FROM = 41.0
+
+
+def tile_picked_ycachep_log_p_kernel(
+    tc, x_words, x_scales, w1_words, w1_scales, w2_words, w2_scales, unit, w3_words, w3_scales, offs, pf, out
+):
+    nc = tc.nc
+    with ExitStack() as ctx:
+        lists = ctx.enter_context(tc.tile_pool(name="lists", bufs=1))
+        keep = ctx.enter_context(tc.tile_pool(name="keep", bufs=1))
+        ring = ctx.enter_context(tc.tile_pool(name="ring", bufs=2))
+        psum = ctx.enter_context(tc.psum_pool(name="psum", bufs=8))
+
+        def load_scale_rows(queue, plane, rows):
+            for q in range(4):
+                queue.dma_start(out=plane[32 * q : 32 * q + 4, :].bitcast(I32), in_=rows[0, 4 * q : 4 * q + 4, :].bitcast(I32))
+
+        offs_t = lists.tile([P, S // 16], U16, name="offs_t")
+        pf_t = lists.tile([P, S // 16], U16, name="pf_t")
+        x_table = keep.tile([P, T], I32, name="x_table", align_bytes=64)
+        x_plane = keep.tile([P, T], U8, name="x_plane", align_bytes=64)
+        w_raw = [keep.tile([P, 2 * H], U8, name="w_raw%d" % s, align_bytes=64) for s in range(2)]
+        ws_raw = [keep.tile([P, H], U8, name="ws_raw%d" % s, align_bytes=64) for s in range(2)]
+        w3_codes = keep.tile([P, 2 * N], U8, name="w3_codes", align_bytes=64)
+        w3_plane = keep.tile([P, N], U8, name="w3_plane", align_bytes=64)
+        unit_t = keep.tile([P, PACK], F32, name="unit_t")
+
+        nc.vector.memset(ws_raw[0][:].bitcast(I32), 0)
+        nc.vector.memset(x_plane[:].bitcast(I32), 0)
+        nc.vector.memset(ws_raw[1][:].bitcast(I32), 0)
+        nc.vector.memset(w3_plane[:].bitcast(I32), 0)
+
+        nc.sync.dma_start(offs_t[:], offs)
+        nc.sync.dma_start(out=w_raw[0][:].bitcast(I32), in_=w1_words[0].bitcast(I32))
+        nc.sync.dma_start(pf_t[:], pf)
+        nc.sync.dma_start(out=w_raw[1][:].bitcast(I32), in_=w2_words[0].bitcast(I32))
+        nc.sync.dma_start(out=x_table[:], in_=x_words[0].rearrange("p n t -> p (n t)").bitcast(I32))
+        load_scale_rows(nc.scalar, ws_raw[0], w1_scales)
+        load_scale_rows(nc.scalar, x_plane, x_scales)
+        load_scale_rows(nc.sync, ws_raw[1], w2_scales)
+        load_scale_rows(nc.sync, w3_plane, w3_scales)
+        nc.gpsimd.dma_start(out=unit_t[:], in_=unit.rearrange("(p t) o -> p (t o)", t=PACK))
+        nc.gpsimd.dma_start(out=w3_codes[:].bitcast(I32), in_=w3_words[0].bitcast(I32))
+
+        w_codes = [keep.tile([P, PACK, 2 * P], U8, name="w_codes%d" % s, align_bytes=64) for s in range(2)]
+        w_plane = [keep.tile([P, PACK, P], U8, name="w_plane%d" % s, align_bytes=64) for s in range(2)]
+
+        def deal_words(s):
+            nc.vector.tensor_copy(
+                out=w_codes[s][:].rearrange("p t (m b) -> p t m b", b=2),
+                in_=w_raw[s][:].rearrange("p (m t b) -> p t m b", t=PACK, b=2),
+            )
+
+        def deal_plane(s):
+            nc.vector.tensor_copy(out=w_plane[s][:], in_=ws_raw[s][:].rearrange("p (m t) -> p t m", t=PACK))
+
+        xg_words = [keep.tile([P, HALF], U32, name="xg_words%d" % h, align_bytes=64) for h in range(2)]
+        xg_plane = [keep.tile([P, HALF], U8, name="xg_plane%d" % h, align_bytes=64) for h in range(2)]
+
+        def entries(lst, h):
+            return lst[:, h * HALF // 16 : (h + 1) * HALF // 16]
+
+        deal_words(0)
+        for h in range(2):
+            nc.vector.tensor_copy(xg_plane[h][:], x_plane[:].indirect(entries(offs_t, h)))
+        deal_plane(0)
+        for h in range(2):
+            nc.vector.tensor_copy(xg_words[h][:], x_table[:].bitcast(U32).indirect(entries(offs_t, h)))
+        deal_words(1)
+        deal_plane(1)
+
+        expo = keep.tile([P, 2 * PACK, S], F32, name="expo")
+        soft = keep.tile([P, 2 * PACK, S], F32, name="soft")
+        for s in range(2):
+            for h in range(2):
+                for t in range(PACK):
+                    acc = psum.tile([P, HALF], F32, name="acc", tag="bank")
+                    nc.tensor.matmul_mx(
+                        out=acc[:],
+                        lhsT=w_codes[s][:, t, :].bitcast(FP4X4),
+                        lhsT_scale=w_plane[s][:, t, :],
+                        rhs=xg_words[h][:].bitcast(FP8X4),
+                        rhs_scale=xg_plane[h][:],
+                        start=True,
+                        stop=True,
+                    )
+                    cols = slice(h * HALF, (h + 1) * HALF)
+                    nc.scalar.activation(out=expo[:, PACK * s + t, cols], in_=acc[:], func=ACT.Exp)
+                    nc.vector.tensor_copy(out=soft[:, PACK * s + t, cols], in_=acc[:])
+
+        cu = keep.tile([P, PACK], F32, name="cu")
+        nc.vector.tensor_scalar(out=cu[:], in0=unit_t[:], scalar1=-0.4, scalar2=None, op0=ALU.mult)
+
+        width = HALF // LN_BLOCKS
+        expo_runs = expo[:].rearrange("p r (h c) -> p (r h) c", h=2)
+        soft_runs = soft[:].rearrange("p r (h c) -> p (r h) c", h=2)
+        for c in range(LN_BLOCKS):
+            cols = slice(c * width, (c + 1) * width)
+            logs = ring.tile([P, 4 * PACK, width], F32, name="logs", bufs=3)
+            nc.scalar.activation(out=logs[:], in_=expo_runs[:, :, cols], func=ACT.Ln, bias=1.0)
+            nc.vector.scalar_tensor_tensor(
+                out=soft_runs[:, :, cols], in0=logs[:], scalar=LINEAR_FROM, in1=soft_runs[:, :, cols], op0=ALU.min, op1=ALU.max
+            )
+
+        inv = [keep.tile([P, S], F32, name="inv%d" % t) for t in range(PACK)]
+        util = [keep.tile([P, S], F32, name="util%d" % t) for t in range(PACK)]
+        util_b = [keep.tile([P, S], F32, name="util_b%d" % t) for t in range(PACK)]
+        marg = [keep.tile([P, S], F32, name="marg%d" % t) for t in range(PACK)]
+        vict = [keep.tile([P, S // D, 1], F32, name="vict%d" % t) for t in range(PACK)]
+        diff = keep.tile([P, PACK, S], F32, name="diff")
+
+        for t in range(PACK):
+            nc.scalar.activation(out=inv[t][:], in_=soft[:, t, :], func=ACT.Abs_reciprocal_sqrt, bias=0.4)
+            nc.scalar.activation(out=inv[t][:], in_=inv[t][:], func=ACT.Square)
+
+        def make_util(t):
+            nc.vector.tensor_tensor(out=util[t][:], in0=soft[:, PACK + t, :], in1=inv[t][:], op=ALU.mult)
+            nc.sync.dma_start(out=util_b[t][:], in_=util[t][:])
+
+        def make_vict(t):
+            sets = util[t][:].rearrange("p (v d) -> p v d", d=D)
+            pair = ring.tile([P, S // D, 2], F32, name="pair")
+            nc.vector.tensor_tensor(out=pair[:], in0=sets[:, :, 0:2], in1=sets[:, :, 2:4], op=ALU.min)
+            nc.vector.tensor_tensor(out=vict[t][:], in0=pair[:, :, 0:1], in1=pair[:, :, 1:2], op=ALU.min)
+            nc.vector.tensor_scalar(out=vict[t][:], in0=vict[t][:], scalar1=unit_t[:, t : t + 1], scalar2=None, op0=ALU.mult)
+
+        def make_marg(t):
+            nc.vector.scalar_tensor_tensor(
+                out=marg[t][:].rearrange("p (v d) -> p v d", d=D),
+                in0=util[t][:].rearrange("p (v d) -> p v d", d=D),
+                scalar=unit_t[:, t : t + 1],
+                in1=vict[t][:].to_broadcast([P, S // D, D]),
+                op0=ALU.mult,
+                op1=ALU.subtract,
+            )
+
+        def make_diff(t):
+            for h in range(2):
+                cols = slice(h * HALF, (h + 1) * HALF)
+                nc.vector.tensor_tensor(
+                    out=diff[:, t, cols], in0=util[t][:].indirect(entries(pf_t, h)), in1=util_b[t][:, cols], op=ALU.subtract
+                )
+            nc.scalar.activation(out=diff[:, t, :], in_=diff[:, t, :], func=ACT.Tanh, scale=0.75)
+
+        make_util(0)
+        make_vict(0)
+        for t in range(1, PACK):
+            make_util(t)
+            make_diff(t - 1)
+        make_vict(1)
+        make_diff(PACK - 1)
+        for t in range(2, PACK):
+            make_vict(t)
+        for t in range(PACK):
+            make_marg(t)
+
+        out_rows = out.rearrange("(b p) j -> p b j", p=P)
+        for c in range(S // OUT_COLS):
+            cols = slice(c * OUT_COLS, (c + 1) * OUT_COLS)
+            ladm = ring.tile([P, PACK, OUT_COLS], F32, name="ladm", bufs=4)
+            nc.scalar.activation(out=ladm[:], in_=diff[:, :, cols], func=ACT.Ln, scale=0.5, bias=0.6)
+            hid = ring.tile([P, PACK, OUT_COLS], BF16, name="hid", align_bytes=64)
+            for t in range(PACK):
+                nc.vector.scalar_tensor_tensor(
+                    out=hid[:, t, :], in0=ladm[:, t, :], scalar=cu[:, t : t + 1], in1=marg[t][:, cols], op0=ALU.mult, op1=ALU.add
+                )
+            woven = ring.tile([P, OUT_COLS, PACK], BF16, name="woven", align_bytes=64)
+            weave = nc.scalar.copy if c < 2 else nc.vector.tensor_copy
+            weave(out=woven[:].rearrange("p (c i) t -> p c t i", i=4), in_=hid[:].rearrange("p t (c i) -> p c t i", i=4))
+            h_codes = ring.tile([P, OUT_COLS], U32, name="h_codes", align_bytes=64)
+            h_plane = ring.tile([P, OUT_COLS], U8, name="h_plane", align_bytes=64)
+            nc.vector.quantize_mx(out=h_codes[:].bitcast(FP8X4), scales=h_plane[:], in_=woven[:].rearrange("p j t -> p (j t)"))
+            acc = psum.tile([P, HALF], F32, name="acc", tag="bank")
+            for b in range(N // P):
+                nc.tensor.matmul_mx(
+                    out=acc[:, b * OUT_COLS : (b + 1) * OUT_COLS],
+                    lhsT=w3_codes[:, 2 * P * b : 2 * P * (b + 1)].bitcast(FP4X4),
+                    lhsT_scale=w3_plane[:, P * b : P * (b + 1)],
+                    rhs=h_codes[:].bitcast(FP8X4),
+                    rhs_scale=h_plane[:],
+                    start=True,
+                    stop=True,
+                )
+            res = ring.tile([P, N // P, OUT_COLS], F32, name="res")
+            nc.scalar.copy(out=res[:].rearrange("p b j -> p (b j)"), in_=acc[:])
+            nc.sync.dma_start(out=out_rows[:, :, cols], in_=res[:])

@@ -20,7 +20,7 @@ P = 128
 PACK = 4
 HALF = 512
 LN_BLOCKS = 8
-OUT_COLS = 256
+OUT_BLOCKS = (256, 256, 256, 128, 128)
 LINEAR_FROM = 41.0
 
 
@@ -32,65 +32,68 @@ def tile_picked_ycachep_log_p_kernel(
         lists = ctx.enter_context(tc.tile_pool(name="lists", bufs=1))
         keep = ctx.enter_context(tc.tile_pool(name="keep", bufs=1))
         ring = ctx.enter_context(tc.tile_pool(name="ring", bufs=2))
+        turns = ctx.enter_context(tc.tile_pool(name="turns", bufs=1))
         psum = ctx.enter_context(tc.psum_pool(name="psum", bufs=8))
 
-        def load_scale_rows(queue, plane, rows):
+        def load_scale_rows(queues, plane, rows):
             for q in range(4):
-                queue.dma_start(out=plane[32 * q : 32 * q + 4, :].bitcast(I32), in_=rows[0, 4 * q : 4 * q + 4, :].bitcast(I32))
+                queues[q].dma_start(out=plane[32 * q : 32 * q + 4, :].bitcast(I32), in_=rows[0, 4 * q : 4 * q + 4, :].bitcast(I32))
 
         offs_t = lists.tile([P, S // 16], U16, name="offs_t")
         pf_t = lists.tile([P, S // 16], U16, name="pf_t")
-        x_table = keep.tile([P, T], I32, name="x_table", align_bytes=64)
-        x_plane = keep.tile([P, T], U8, name="x_plane", align_bytes=64)
-        w_raw = [keep.tile([P, 2 * H], U8, name="w_raw%d" % s, align_bytes=64) for s in range(2)]
-        ws_raw = [keep.tile([P, H], U8, name="ws_raw%d" % s, align_bytes=64) for s in range(2)]
-        w3_codes = keep.tile([P, 2 * N], U8, name="w3_codes", align_bytes=64)
-        w3_plane = keep.tile([P, N], U8, name="w3_plane", align_bytes=64)
-        unit_t = keep.tile([P, PACK], F32, name="unit_t")
+        x_table = keep.tile([P, T], I32, name="x_table", tag="table", align_bytes=64)
+        x_plane = turns.tile([P, T], U8, name="x_plane", align_bytes=64, offset=0)
+        w1_raw = keep.tile([P, 3 * H], U8, name="w1_raw", tag="w1_raw", align_bytes=64)
+        w2_raw = keep.tile([P, 2 * H], U8, name="w2_raw", align_bytes=64)
+        w1_rows = w1_raw[:, 2 * H : 3 * H]
 
-        nc.vector.memset(ws_raw[0][:].bitcast(I32), 0)
         nc.vector.memset(x_plane[:].bitcast(I32), 0)
-        nc.vector.memset(ws_raw[1][:].bitcast(I32), 0)
-        nc.vector.memset(w3_plane[:].bitcast(I32), 0)
+        nc.vector.memset(w1_rows.bitcast(I32), 0)
 
         nc.sync.dma_start(offs_t[:], offs)
-        nc.sync.dma_start(out=w_raw[0][:].bitcast(I32), in_=w1_words[0].bitcast(I32))
+        nc.sync.dma_start(out=w1_raw[:, 0 : 2 * H].bitcast(I32), in_=w1_words[0].bitcast(I32))
         nc.sync.dma_start(pf_t[:], pf)
-        nc.sync.dma_start(out=w_raw[1][:].bitcast(I32), in_=w2_words[0].bitcast(I32))
         nc.sync.dma_start(out=x_table[:], in_=x_words[0].rearrange("p n t -> p (n t)").bitcast(I32))
-        load_scale_rows(nc.scalar, ws_raw[0], w1_scales)
-        load_scale_rows(nc.scalar, x_plane, x_scales)
-        load_scale_rows(nc.sync, ws_raw[1], w2_scales)
-        load_scale_rows(nc.sync, w3_plane, w3_scales)
-        nc.gpsimd.dma_start(out=unit_t[:], in_=unit.rearrange("(p t) o -> p (t o)", t=PACK))
-        nc.gpsimd.dma_start(out=w3_codes[:].bitcast(I32), in_=w3_words[0].bitcast(I32))
+        nc.gpsimd.dma_start(out=w2_raw[:].bitcast(I32), in_=w2_words[0].bitcast(I32))
+        load_scale_rows([nc.scalar] * 4, x_plane, x_scales)
+        load_scale_rows([nc.gpsimd] + [nc.scalar] * 3, w1_rows, w1_scales)
 
         w_codes = [keep.tile([P, PACK, 2 * P], U8, name="w_codes%d" % s, align_bytes=64) for s in range(2)]
         w_plane = [keep.tile([P, PACK, P], U8, name="w_plane%d" % s, align_bytes=64) for s in range(2)]
 
-        def deal_words(s):
+        def deal_words(s, raw):
             nc.vector.tensor_copy(
                 out=w_codes[s][:].rearrange("p t (m b) -> p t m b", b=2),
-                in_=w_raw[s][:].rearrange("p (m t b) -> p t m b", t=PACK, b=2),
+                in_=raw.rearrange("p (m t b) -> p t m b", t=PACK, b=2),
             )
 
-        def deal_plane(s):
-            nc.vector.tensor_copy(out=w_plane[s][:], in_=ws_raw[s][:].rearrange("p (m t) -> p t m", t=PACK))
+        def deal_plane(s, rows):
+            nc.vector.tensor_copy(out=w_plane[s][:], in_=rows.rearrange("p (m t) -> p t m", t=PACK))
 
-        xg_words = [keep.tile([P, HALF], U32, name="xg_words%d" % h, align_bytes=64) for h in range(2)]
         xg_plane = [keep.tile([P, HALF], U8, name="xg_plane%d" % h, align_bytes=64) for h in range(2)]
 
         def entries(lst, h):
             return lst[:, h * HALF // 16 : (h + 1) * HALF // 16]
 
-        deal_words(0)
+        deal_words(0, w1_raw[:, 0 : 2 * H])
+        deal_plane(0, w1_rows)
         for h in range(2):
             nc.vector.tensor_copy(xg_plane[h][:], x_plane[:].indirect(entries(offs_t, h)))
-        deal_plane(0)
+        xg_words = [
+            turns.tile([P, HALF], U32, name="xg_words0", align_bytes=64, offset=0),
+            keep.tile([P, HALF], U32, name="xg_words1", tag="w1_raw", align_bytes=64),
+        ]
+        late_rows = turns.tile([P, H], U8, name="late_rows", align_bytes=64, offset=4 * HALF)
+        nc.gpsimd.memset(late_rows[:].bitcast(I32), 0)
+        load_scale_rows([nc.sync] * 4, late_rows, w2_scales)
         for h in range(2):
             nc.vector.tensor_copy(xg_words[h][:], x_table[:].bitcast(U32).indirect(entries(offs_t, h)))
-        deal_words(1)
-        deal_plane(1)
+        deal_words(1, w2_raw[:])
+        deal_plane(1, late_rows[:])
+        w3_plane = late_rows[:, 0:N]
+        load_scale_rows([nc.sync] * 4, w3_plane, w3_scales)
+        unit_t = keep.tile([P, PACK], F32, name="unit_t", tag="table", align_bytes=64)
+        nc.sync.dma_start(out=unit_t[:], in_=unit.rearrange("(p t) o -> p (t o)", t=PACK))
 
         expo = keep.tile([P, 2 * PACK, S], F32, name="expo")
         soft = keep.tile([P, 2 * PACK, S], F32, name="soft")
@@ -111,6 +114,8 @@ def tile_picked_ycachep_log_p_kernel(
                     nc.scalar.activation(out=expo[:, PACK * s + t, cols], in_=acc[:], func=ACT.Exp)
                     nc.vector.tensor_copy(out=soft[:, PACK * s + t, cols], in_=acc[:])
 
+        w3_codes = turns.tile([P, 2 * N], U8, name="w3_codes", align_bytes=64, offset=0)
+        nc.sync.dma_start(out=w3_codes[:].bitcast(I32), in_=w3_words[0].bitcast(I32))
         cu = keep.tile([P, PACK], F32, name="cu")
         nc.vector.tensor_scalar(out=cu[:], in0=unit_t[:], scalar1=-0.4, scalar2=None, op0=ALU.mult)
 
@@ -127,25 +132,28 @@ def tile_picked_ycachep_log_p_kernel(
 
         inv = [keep.tile([P, S], F32, name="inv%d" % t) for t in range(PACK)]
         util = [keep.tile([P, S], F32, name="util%d" % t) for t in range(PACK)]
-        util_b = [keep.tile([P, S], F32, name="util_b%d" % t) for t in range(PACK)]
+        util_b = [keep.tile([P, S], F32, name="util_b%d" % t) for t in range(PACK - 1)]
         marg = [keep.tile([P, S], F32, name="marg%d" % t) for t in range(PACK)]
         vict = [keep.tile([P, S // D, 1], F32, name="vict%d" % t) for t in range(PACK)]
         diff = keep.tile([P, PACK, S], F32, name="diff")
 
         for t in range(PACK):
             nc.scalar.activation(out=inv[t][:], in_=soft[:, t, :], func=ACT.Abs_reciprocal_sqrt, bias=0.4)
-            nc.scalar.activation(out=inv[t][:], in_=inv[t][:], func=ACT.Square)
+            if t > 0:
+                nc.scalar.activation(out=inv[t][:], in_=inv[t][:], func=ACT.Square)
 
         def make_util(t):
+            if t == 0:
+                nc.vector.tensor_tensor(out=soft[:, PACK, :], in0=soft[:, PACK, :], in1=inv[0][:], op=ALU.mult)
             nc.vector.tensor_tensor(out=util[t][:], in0=soft[:, PACK + t, :], in1=inv[t][:], op=ALU.mult)
-            nc.sync.dma_start(out=util_b[t][:], in_=util[t][:])
+            if t < PACK - 1:
+                nc.sync.dma_start(out=util_b[t][:], in_=util[t][:])
 
         def make_vict(t):
             sets = util[t][:].rearrange("p (v d) -> p v d", d=D)
-            pair = ring.tile([P, S // D, 2], F32, name="pair")
-            nc.vector.tensor_tensor(out=pair[:], in0=sets[:, :, 0:2], in1=sets[:, :, 2:4], op=ALU.min)
-            nc.vector.tensor_tensor(out=vict[t][:], in0=pair[:, :, 0:1], in1=pair[:, :, 1:2], op=ALU.min)
-            nc.vector.tensor_scalar(out=vict[t][:], in0=vict[t][:], scalar1=unit_t[:, t : t + 1], scalar2=None, op0=ALU.mult)
+            flat = vict[t][:].rearrange("p v o -> p (v o)")
+            nc.vector.tensor_reduce(out=flat, in_=sets, axis=mybir.AxisListType.X, op=ALU.min)
+            nc.scalar.activation(out=flat, in_=flat, func=ACT.Copy, scale=unit_t[:, t : t + 1])
 
         def make_marg(t):
             nc.vector.scalar_tensor_tensor(
@@ -163,40 +171,52 @@ def tile_picked_ycachep_log_p_kernel(
                 nc.vector.tensor_tensor(
                     out=diff[:, t, cols], in0=util[t][:].indirect(entries(pf_t, h)), in1=util_b[t][:, cols], op=ALU.subtract
                 )
+
+        def fetch_on_scalar(t):
+            for h in range(2):
+                cols = slice(h * HALF, (h + 1) * HALF)
+                nc.scalar.activation(out=diff[:, t, cols], in_=util[t][:].indirect(entries(pf_t, h)), func=ACT.Copy)
+
+        def make_tanh(t):
             nc.scalar.activation(out=diff[:, t, :], in_=diff[:, t, :], func=ACT.Tanh, scale=0.75)
 
-        make_util(0)
-        make_vict(0)
-        for t in range(1, PACK):
+        last = PACK - 1
+        for t in range(PACK):
             make_util(t)
-            make_diff(t - 1)
-        make_vict(1)
-        make_diff(PACK - 1)
-        for t in range(2, PACK):
+        make_diff(0)
+        make_tanh(0)
+        fetch_on_scalar(last)
+        for t in range(1, last):
+            make_diff(t)
+            make_tanh(t)
+        nc.vector.tensor_tensor(out=diff[:, last, :], in0=diff[:, last, :], in1=util[last][:], op=ALU.subtract)
+        make_tanh(last)
+        for t in range(PACK):
             make_vict(t)
         for t in range(PACK):
             make_marg(t)
 
         out_rows = out.rearrange("(b p) j -> p b j", p=P)
-        for c in range(S // OUT_COLS):
-            cols = slice(c * OUT_COLS, (c + 1) * OUT_COLS)
-            ladm = ring.tile([P, PACK, OUT_COLS], F32, name="ladm", bufs=4)
+        for c, wide in enumerate(OUT_BLOCKS):
+            first = sum(OUT_BLOCKS[:c])
+            cols = slice(first, first + wide)
+            ladm = ring.tile([P, PACK, wide], F32, name="ladm", bufs=5)
             nc.scalar.activation(out=ladm[:], in_=diff[:, :, cols], func=ACT.Ln, scale=0.5, bias=0.6)
-            hid = ring.tile([P, PACK, OUT_COLS], BF16, name="hid", align_bytes=64)
+            hid = ring.tile([P, PACK, wide], BF16, name="hid", align_bytes=64)
             for t in range(PACK):
                 nc.vector.scalar_tensor_tensor(
                     out=hid[:, t, :], in0=ladm[:, t, :], scalar=cu[:, t : t + 1], in1=marg[t][:, cols], op0=ALU.mult, op1=ALU.add
                 )
-            woven = ring.tile([P, OUT_COLS, PACK], BF16, name="woven", align_bytes=64)
-            weave = nc.scalar.copy if c < 2 else nc.vector.tensor_copy
+            woven = ring.tile([P, wide, PACK], BF16, name="woven", align_bytes=64)
+            weave = nc.scalar.copy if c < 3 else nc.vector.tensor_copy
             weave(out=woven[:].rearrange("p (c i) t -> p c t i", i=4), in_=hid[:].rearrange("p t (c i) -> p c t i", i=4))
-            h_codes = ring.tile([P, OUT_COLS], U32, name="h_codes", align_bytes=64)
-            h_plane = ring.tile([P, OUT_COLS], U8, name="h_plane", align_bytes=64)
+            h_codes = ring.tile([P, wide], U32, name="h_codes", align_bytes=64)
+            h_plane = ring.tile([P, wide], U8, name="h_plane", align_bytes=64)
             nc.vector.quantize_mx(out=h_codes[:].bitcast(FP8X4), scales=h_plane[:], in_=woven[:].rearrange("p j t -> p (j t)"))
             acc = psum.tile([P, HALF], F32, name="acc", tag="bank")
             for b in range(N // P):
                 nc.tensor.matmul_mx(
-                    out=acc[:, b * OUT_COLS : (b + 1) * OUT_COLS],
+                    out=acc[:, b * wide : (b + 1) * wide],
                     lhsT=w3_codes[:, 2 * P * b : 2 * P * (b + 1)].bitcast(FP4X4),
                     lhsT_scale=w3_plane[:, P * b : P * (b + 1)],
                     rhs=h_codes[:].bitcast(FP8X4),
@@ -204,6 +224,6 @@ def tile_picked_ycachep_log_p_kernel(
                     start=True,
                     stop=True,
                 )
-            res = ring.tile([P, N // P, OUT_COLS], F32, name="res")
-            nc.scalar.copy(out=res[:].rearrange("p b j -> p (b j)"), in_=acc[:])
+            res = ring.tile([P, N // P, wide], F32, name="res")
+            nc.scalar.copy(out=res[:].rearrange("p b j -> p (b j)"), in_=acc[:, 0 : 2 * wide])
             nc.sync.dma_start(out=out_rows[:, :, cols], in_=res[:])

@@ -35,28 +35,29 @@ def tile_picked_ycachep_log_p_kernel(
         turns = ctx.enter_context(tc.tile_pool(name="turns", bufs=1))
         psum = ctx.enter_context(tc.psum_pool(name="psum", bufs=8))
 
-        def load_scale_rows(queues, plane, rows):
+        def load_scale_rows(plane, rows):
             for q in range(4):
-                queues[q].dma_start(out=plane[32 * q : 32 * q + 4, :].bitcast(I32), in_=rows[0, 4 * q : 4 * q + 4, :].bitcast(I32))
+                nc.sync.dma_start(out=plane[32 * q : 32 * q + 4, :].bitcast(I32), in_=rows[0, 4 * q : 4 * q + 4, :].bitcast(I32))
 
         offs_t = lists.tile([P, S // 16], U16, name="offs_t")
         pf_t = lists.tile([P, S // 16], U16, name="pf_t")
         x_table = keep.tile([P, T], I32, name="x_table", tag="table", align_bytes=64)
         x_plane = turns.tile([P, T], U8, name="x_plane", align_bytes=64, offset=0)
         w1_raw = keep.tile([P, 3 * H], U8, name="w1_raw", tag="w1_raw", align_bytes=64)
-        w2_raw = keep.tile([P, 2 * H], U8, name="w2_raw", align_bytes=64)
         w1_rows = w1_raw[:, 2 * H : 3 * H]
 
-        nc.vector.memset(x_plane[:].bitcast(I32), 0)
+        nc.vector.memset(x_plane[:, 0 : T // 2].bitcast(I32), 0)
+        nc.gpsimd.memset(x_plane[:, T // 2 : T].bitcast(I32), 0)
         nc.vector.memset(w1_rows.bitcast(I32), 0)
 
         nc.sync.dma_start(offs_t[:], offs)
-        nc.sync.dma_start(out=w1_raw[:, 0 : 2 * H].bitcast(I32), in_=w1_words[0].bitcast(I32))
+        nc.scalar.dma_start(out=w1_raw[:, 0 : 2 * H].bitcast(I32), in_=w1_words[0].bitcast(I32))
+        x_rows = x_words[0].rearrange("p n t -> p (n t)").bitcast(I32)
+        nc.sync.dma_start(out=x_table[:, 0 : T // 2], in_=x_rows[:, 0 : T // 2])
+        load_scale_rows(x_plane, x_scales)
+        nc.sync.dma_start(out=x_table[:, T // 2 : T], in_=x_rows[:, T // 2 : T])
         nc.sync.dma_start(pf_t[:], pf)
-        nc.sync.dma_start(out=x_table[:], in_=x_words[0].rearrange("p n t -> p (n t)").bitcast(I32))
-        nc.gpsimd.dma_start(out=w2_raw[:].bitcast(I32), in_=w2_words[0].bitcast(I32))
-        load_scale_rows([nc.scalar] * 4, x_plane, x_scales)
-        load_scale_rows([nc.gpsimd] + [nc.scalar] * 3, w1_rows, w1_scales)
+        load_scale_rows(w1_rows, w1_scales)
 
         w_codes = [keep.tile([P, PACK, 2 * P], U8, name="w_codes%d" % s, align_bytes=64) for s in range(2)]
         w_plane = [keep.tile([P, PACK, P], U8, name="w_plane%d" % s, align_bytes=64) for s in range(2)]
@@ -84,14 +85,16 @@ def tile_picked_ycachep_log_p_kernel(
             keep.tile([P, HALF], U32, name="xg_words1", tag="w1_raw", align_bytes=64),
         ]
         late_rows = turns.tile([P, H], U8, name="late_rows", align_bytes=64, offset=4 * HALF)
+        w2_raw = turns.tile([P, 2 * H], U8, name="w2_raw", align_bytes=64, offset=4 * HALF + H)
+        nc.sync.dma_start(out=w2_raw[:].bitcast(I32), in_=w2_words[0].bitcast(I32))
         nc.gpsimd.memset(late_rows[:].bitcast(I32), 0)
-        load_scale_rows([nc.sync] * 4, late_rows, w2_scales)
+        load_scale_rows(late_rows, w2_scales)
         for h in range(2):
             nc.vector.tensor_copy(xg_words[h][:], x_table[:].bitcast(U32).indirect(entries(offs_t, h)))
         deal_words(1, w2_raw[:])
         deal_plane(1, late_rows[:])
         w3_plane = late_rows[:, 0:N]
-        load_scale_rows([nc.sync] * 4, w3_plane, w3_scales)
+        load_scale_rows(w3_plane, w3_scales)
         unit_t = keep.tile([P, PACK], F32, name="unit_t", tag="table", align_bytes=64)
         nc.sync.dma_start(out=unit_t[:], in_=unit.rearrange("(p t) o -> p (t o)", t=PACK))
 
@@ -133,18 +136,19 @@ def tile_picked_ycachep_log_p_kernel(
         inv = [keep.tile([P, S], F32, name="inv%d" % t) for t in range(PACK)]
         util = [keep.tile([P, S], F32, name="util%d" % t) for t in range(PACK)]
         util_b = [keep.tile([P, S], F32, name="util_b%d" % t) for t in range(PACK - 1)]
-        marg = [keep.tile([P, S], F32, name="marg%d" % t) for t in range(PACK)]
+        marg = inv
         vict = [keep.tile([P, S // D, 1], F32, name="vict%d" % t) for t in range(PACK)]
         diff = keep.tile([P, PACK, S], F32, name="diff")
 
-        for t in range(PACK):
+        for h in range(2):
+            cols = slice(h * HALF, (h + 1) * HALF)
+            nc.scalar.activation(out=inv[0][:, cols], in_=soft[:, 0, cols], func=ACT.Abs_reciprocal_sqrt, bias=0.4)
+            nc.vector.tensor_tensor(out=soft[:, PACK, cols], in0=soft[:, PACK, cols], in1=inv[0][:, cols], op=ALU.mult)
+        for t in range(1, PACK):
             nc.scalar.activation(out=inv[t][:], in_=soft[:, t, :], func=ACT.Abs_reciprocal_sqrt, bias=0.4)
-            if t > 0:
-                nc.scalar.activation(out=inv[t][:], in_=inv[t][:], func=ACT.Square)
+            nc.scalar.activation(out=inv[t][:], in_=inv[t][:], func=ACT.Square)
 
         def make_util(t):
-            if t == 0:
-                nc.vector.tensor_tensor(out=soft[:, PACK, :], in0=soft[:, PACK, :], in1=inv[0][:], op=ALU.mult)
             nc.vector.tensor_tensor(out=util[t][:], in0=soft[:, PACK + t, :], in1=inv[t][:], op=ALU.mult)
             if t < PACK - 1:
                 nc.sync.dma_start(out=util_b[t][:], in_=util[t][:])
@@ -152,7 +156,9 @@ def tile_picked_ycachep_log_p_kernel(
         def make_vict(t):
             sets = util[t][:].rearrange("p (v d) -> p v d", d=D)
             flat = vict[t][:].rearrange("p v o -> p (v o)")
-            nc.vector.tensor_reduce(out=flat, in_=sets, axis=mybir.AxisListType.X, op=ALU.min)
+            pair = ring.tile([P, S // D, 2], F32, name="pair")
+            nc.vector.tensor_tensor(out=pair[:], in0=sets[:, :, 0:2], in1=sets[:, :, 2:4], op=ALU.min)
+            nc.vector.tensor_tensor(out=vict[t][:], in0=pair[:, :, 0:1], in1=pair[:, :, 1:2], op=ALU.min)
             nc.scalar.activation(out=flat, in_=flat, func=ACT.Copy, scale=unit_t[:, t : t + 1])
 
         def make_marg(t):
@@ -202,16 +208,16 @@ def tile_picked_ycachep_log_p_kernel(
             cols = slice(first, first + wide)
             ladm = ring.tile([P, PACK, wide], F32, name="ladm", bufs=5)
             nc.scalar.activation(out=ladm[:], in_=diff[:, :, cols], func=ACT.Ln, scale=0.5, bias=0.6)
-            hid = ring.tile([P, PACK, wide], BF16, name="hid", align_bytes=64)
+            hid = ring.tile([P, PACK, wide], BF16, name="hid", bufs=3, align_bytes=64)
             for t in range(PACK):
                 nc.vector.scalar_tensor_tensor(
                     out=hid[:, t, :], in0=ladm[:, t, :], scalar=cu[:, t : t + 1], in1=marg[t][:, cols], op0=ALU.mult, op1=ALU.add
                 )
-            woven = ring.tile([P, wide, PACK], BF16, name="woven", align_bytes=64)
-            weave = nc.scalar.copy if c < 3 else nc.vector.tensor_copy
+            woven = ring.tile([P, wide, PACK], BF16, name="woven", bufs=3, align_bytes=64)
+            weave = nc.scalar.copy if c < 2 else nc.vector.tensor_copy
             weave(out=woven[:].rearrange("p (c i) t -> p c t i", i=4), in_=hid[:].rearrange("p t (c i) -> p c t i", i=4))
-            h_codes = ring.tile([P, wide], U32, name="h_codes", align_bytes=64)
-            h_plane = ring.tile([P, wide], U8, name="h_plane", align_bytes=64)
+            h_codes = ring.tile([P, wide], U32, name="h_codes", bufs=3, align_bytes=64)
+            h_plane = ring.tile([P, wide], U8, name="h_plane", bufs=3, align_bytes=64)
             nc.vector.quantize_mx(out=h_codes[:].bitcast(FP8X4), scales=h_plane[:], in_=woven[:].rearrange("p j t -> p (j t)"))
             acc = psum.tile([P, HALF], F32, name="acc", tag="bank")
             for b in range(N // P):
@@ -224,6 +230,6 @@ def tile_picked_ycachep_log_p_kernel(
                     start=True,
                     stop=True,
                 )
-            res = ring.tile([P, N // P, wide], F32, name="res")
+            res = ring.tile([P, N // P, wide], F32, name="res", bufs=5)
             nc.scalar.copy(out=res[:].rearrange("p b j -> p (b j)"), in_=acc[:, 0 : 2 * wide])
             nc.sync.dma_start(out=out_rows[:, :, cols], in_=res[:])

@@ -18,10 +18,15 @@ ALU = mybir.AluOpType
 
 P = 128
 PACK = 4
-HALF = 512
-LN_BLOCKS = 8
-OUT_BLOCKS = (256, 256, 256, 128, 128)
+HALF = S // 2
+RECY, FREQ = 0, 1
+
 LINEAR_FROM = 41.0
+
+OUT_BLOCKS = (256, 256, 256, 128, 128)
+
+SCALAR_FETCHES = 3
+SCALAR_WEAVES = 2
 
 
 def tile_picked_ycachep_log_p_kernel(
@@ -39,129 +44,152 @@ def tile_picked_ycachep_log_p_kernel(
             for q in range(4):
                 nc.sync.dma_start(out=plane[32 * q : 32 * q + 4, :].bitcast(I32), in_=rows[0, 4 * q : 4 * q + 4, :].bitcast(I32))
 
+        def columns(h):
+            return slice(h * HALF, (h + 1) * HALF)
+
+        def entries(list_tile, h):
+            return list_tile[:, h * HALF // 16 : (h + 1) * HALF // 16]
+
         offs_t = lists.tile([P, S // 16], U16, name="offs_t")
         pf_t = lists.tile([P, S // 16], U16, name="pf_t")
         x_table = keep.tile([P, T], I32, name="x_table", tag="table", align_bytes=64)
         x_plane = turns.tile([P, T], U8, name="x_plane", align_bytes=64, offset=0)
         w1_raw = keep.tile([P, 3 * H], U8, name="w1_raw", tag="w1_raw", align_bytes=64)
-        w1_rows = w1_raw[:, 2 * H : 3 * H]
+        w1_raw_words = w1_raw[:, 0 : 2 * H]
+        w1_raw_plane = w1_raw[:, 2 * H : 3 * H]
 
         nc.vector.memset(x_plane[:, 0 : T // 2].bitcast(I32), 0)
         nc.gpsimd.memset(x_plane[:, T // 2 : T].bitcast(I32), 0)
-        nc.vector.memset(w1_rows.bitcast(I32), 0)
+        nc.vector.memset(w1_raw_plane.bitcast(I32), 0)
 
         nc.sync.dma_start(offs_t[:], offs)
-        nc.scalar.dma_start(out=w1_raw[:, 0 : 2 * H].bitcast(I32), in_=w1_words[0].bitcast(I32))
+        nc.scalar.dma_start(out=w1_raw_words.bitcast(I32), in_=w1_words[0].bitcast(I32))
         x_rows = x_words[0].rearrange("p n t -> p (n t)").bitcast(I32)
         nc.sync.dma_start(out=x_table[:, 0 : T // 2], in_=x_rows[:, 0 : T // 2])
         load_scale_rows(x_plane, x_scales)
         nc.sync.dma_start(out=x_table[:, T // 2 : T], in_=x_rows[:, T // 2 : T])
         nc.sync.dma_start(pf_t[:], pf)
-        load_scale_rows(w1_rows, w1_scales)
+        load_scale_rows(w1_raw_plane, w1_scales)
 
-        w_codes = [keep.tile([P, PACK, 2 * P], U8, name="w_codes%d" % s, align_bytes=64) for s in range(2)]
-        w_plane = [keep.tile([P, PACK, P], U8, name="w_plane%d" % s, align_bytes=64) for s in range(2)]
+        w_codes = [keep.tile([P, PACK, 2 * P], U8, name="w_codes%d" % side, align_bytes=64) for side in (RECY, FREQ)]
+        w_plane = [keep.tile([P, PACK, P], U8, name="w_plane%d" % side, align_bytes=64) for side in (RECY, FREQ)]
 
-        def deal_words(s, raw):
+        def deal(side, raw_words, raw_plane):
             nc.vector.tensor_copy(
-                out=w_codes[s][:].rearrange("p t (m b) -> p t m b", b=2),
-                in_=raw.rearrange("p (m t b) -> p t m b", t=PACK, b=2),
+                out=w_codes[side][:].rearrange("p t (m b) -> p t m b", b=2),
+                in_=raw_words.rearrange("p (m t b) -> p t m b", t=PACK, b=2),
             )
-
-        def deal_plane(s, rows):
-            nc.vector.tensor_copy(out=w_plane[s][:], in_=rows.rearrange("p (m t) -> p t m", t=PACK))
+            nc.vector.tensor_copy(out=w_plane[side][:], in_=raw_plane.rearrange("p (m t) -> p t m", t=PACK))
 
         xg_plane = [keep.tile([P, HALF], U8, name="xg_plane%d" % h, align_bytes=64) for h in range(2)]
-
-        def entries(lst, h):
-            return lst[:, h * HALF // 16 : (h + 1) * HALF // 16]
-
-        deal_words(0, w1_raw[:, 0 : 2 * H])
-        deal_plane(0, w1_rows)
+        deal(RECY, w1_raw_words, w1_raw_plane)
         for h in range(2):
             nc.vector.tensor_copy(xg_plane[h][:], x_plane[:].indirect(entries(offs_t, h)))
+
         xg_words = [
             turns.tile([P, HALF], U32, name="xg_words0", align_bytes=64, offset=0),
             keep.tile([P, HALF], U32, name="xg_words1", tag="w1_raw", align_bytes=64),
         ]
-        late_rows = turns.tile([P, H], U8, name="late_rows", align_bytes=64, offset=4 * HALF)
-        w2_raw = turns.tile([P, 2 * H], U8, name="w2_raw", align_bytes=64, offset=4 * HALF + H)
-        nc.sync.dma_start(out=w2_raw[:].bitcast(I32), in_=w2_words[0].bitcast(I32))
-        nc.gpsimd.memset(late_rows[:].bitcast(I32), 0)
-        load_scale_rows(late_rows, w2_scales)
+        late_plane = turns.tile([P, H], U8, name="late_plane", align_bytes=64, offset=4 * HALF)
+        w2_raw_words = turns.tile([P, 2 * H], U8, name="w2_raw_words", align_bytes=64, offset=4 * HALF + H)
+        nc.sync.dma_start(out=w2_raw_words[:].bitcast(I32), in_=w2_words[0].bitcast(I32))
+        nc.gpsimd.memset(late_plane[:].bitcast(I32), 0)
+        load_scale_rows(late_plane, w2_scales)
         for h in range(2):
             nc.vector.tensor_copy(xg_words[h][:], x_table[:].bitcast(U32).indirect(entries(offs_t, h)))
-        deal_words(1, w2_raw[:])
-        deal_plane(1, late_rows[:])
-        w3_plane = late_rows[:, 0:N]
+        deal(FREQ, w2_raw_words[:], late_plane[:])
+
+        w3_plane = late_plane[:, 0:N]
         load_scale_rows(w3_plane, w3_scales)
         unit_t = keep.tile([P, PACK], F32, name="unit_t", tag="table", align_bytes=64)
         nc.sync.dma_start(out=unit_t[:], in_=unit.rearrange("(p t) o -> p (t o)", t=PACK))
 
         expo = keep.tile([P, 2 * PACK, S], F32, name="expo")
         soft = keep.tile([P, 2 * PACK, S], F32, name="soft")
-        for s in range(2):
+        freq_banks = {}
+        for side in (RECY, FREQ):
             for h in range(2):
                 for t in range(PACK):
-                    acc = psum.tile([P, HALF], F32, name="acc", tag="bank")
+                    product = psum.tile([P, HALF], F32, name="product", tag="bank")
                     nc.tensor.matmul_mx(
-                        out=acc[:],
-                        lhsT=w_codes[s][:, t, :].bitcast(FP4X4),
-                        lhsT_scale=w_plane[s][:, t, :],
+                        out=product[:],
+                        lhsT=w_codes[side][:, t, :].bitcast(FP4X4),
+                        lhsT_scale=w_plane[side][:, t, :],
                         rhs=xg_words[h][:].bitcast(FP8X4),
                         rhs_scale=xg_plane[h][:],
                         start=True,
                         stop=True,
                     )
-                    cols = slice(h * HALF, (h + 1) * HALF)
-                    nc.scalar.activation(out=expo[:, PACK * s + t, cols], in_=acc[:], func=ACT.Exp)
-                    nc.vector.tensor_copy(out=soft[:, PACK * s + t, cols], in_=acc[:])
+                    nc.scalar.activation(out=expo[:, PACK * side + t, columns(h)], in_=product[:], func=ACT.Exp)
+                    if side == RECY:
+                        nc.vector.tensor_copy(out=soft[:, t, columns(h)], in_=product[:])
+                    else:
+                        freq_banks[t, h] = product
 
         w3_codes = turns.tile([P, 2 * N], U8, name="w3_codes", align_bytes=64, offset=0)
         nc.sync.dma_start(out=w3_codes[:].bitcast(I32), in_=w3_words[0].bitcast(I32))
-        cu = keep.tile([P, PACK], F32, name="cu")
-        nc.vector.tensor_scalar(out=cu[:], in0=unit_t[:], scalar1=-0.4, scalar2=None, op0=ALU.mult)
+        log_weight = keep.tile([P, PACK], F32, name="log_weight")
+        nc.vector.tensor_scalar(out=log_weight[:], in0=unit_t[:], scalar1=-0.4, scalar2=None, op0=ALU.mult)
 
-        width = HALF // LN_BLOCKS
-        expo_runs = expo[:].rearrange("p r (h c) -> p (r h) c", h=2)
-        soft_runs = soft[:].rearrange("p r (h c) -> p (r h) c", h=2)
-        for c in range(LN_BLOCKS):
-            cols = slice(c * width, (c + 1) * width)
-            logs = ring.tile([P, 4 * PACK, width], F32, name="logs", bufs=3)
-            nc.scalar.activation(out=logs[:], in_=expo_runs[:, :, cols], func=ACT.Ln, bias=1.0)
+        def bounded(row, cols, product):
             nc.vector.scalar_tensor_tensor(
-                out=soft_runs[:, :, cols], in0=logs[:], scalar=LINEAR_FROM, in1=soft_runs[:, :, cols], op0=ALU.min, op1=ALU.max
+                out=soft[:, row, cols], in0=expo[:, row, cols], scalar=LINEAR_FROM, in1=product, op0=ALU.min, op1=ALU.max
             )
 
-        inv = [keep.tile([P, S], F32, name="inv%d" % t) for t in range(PACK)]
+        for t in range(PACK):
+            nc.scalar.activation(out=expo[:, t, :], in_=expo[:, t, :], func=ACT.Ln, bias=1.0)
+            bounded(t, slice(0, S), soft[:, t, :])
+        for t in range(PACK):
+            nc.scalar.activation(out=expo[:, PACK + t, :], in_=expo[:, PACK + t, :], func=ACT.Ln, bias=1.0)
+            for h in range(2):
+                bounded(PACK + t, columns(h), freq_banks[t, h][:])
+
+        factor = [keep.tile([P, S], F32, name="factor%d" % t, tag="factor%d" % t) for t in range(PACK)]
         util = [keep.tile([P, S], F32, name="util%d" % t) for t in range(PACK)]
-        util_b = [keep.tile([P, S], F32, name="util_b%d" % t) for t in range(PACK - 1)]
-        marg = inv
-        vict = [keep.tile([P, S // D, 1], F32, name="vict%d" % t) for t in range(PACK)]
-        diff = keep.tile([P, PACK, S], F32, name="diff")
-
         for h in range(2):
-            cols = slice(h * HALF, (h + 1) * HALF)
-            nc.scalar.activation(out=inv[0][:, cols], in_=soft[:, 0, cols], func=ACT.Abs_reciprocal_sqrt, bias=0.4)
-            nc.vector.tensor_tensor(out=soft[:, PACK, cols], in0=soft[:, PACK, cols], in1=inv[0][:, cols], op=ALU.mult)
+            cols = columns(h)
+            nc.scalar.activation(out=factor[0][:, cols], in_=soft[:, 0, cols], func=ACT.Abs_reciprocal_sqrt, bias=0.4)
+            nc.vector.tensor_tensor(out=soft[:, PACK, cols], in0=soft[:, PACK, cols], in1=factor[0][:, cols], op=ALU.mult)
         for t in range(1, PACK):
-            nc.scalar.activation(out=inv[t][:], in_=soft[:, t, :], func=ACT.Abs_reciprocal_sqrt, bias=0.4)
-            nc.scalar.activation(out=inv[t][:], in_=inv[t][:], func=ACT.Square)
+            nc.scalar.activation(out=factor[t][:], in_=soft[:, t, :], func=ACT.Abs_reciprocal_sqrt, bias=0.4)
+            nc.scalar.activation(out=factor[t][:], in_=factor[t][:], func=ACT.Square)
 
-        def make_util(t):
-            nc.vector.tensor_tensor(out=util[t][:], in0=soft[:, PACK + t, :], in1=inv[t][:], op=ALU.mult)
-            if t < PACK - 1:
-                nc.sync.dma_start(out=util_b[t][:], in_=util[t][:])
+        halves = [(t, h) for t in range(PACK) for h in range(2)]
+        on_vector, on_scalar = halves[:-SCALAR_FETCHES], halves[-SCALAR_FETCHES:]
+        gap = keep.tile([P, PACK, S], F32, name="gap")
+        util_copy = {}
+        for t in range(PACK):
+            nc.vector.tensor_tensor(out=util[t][:], in0=soft[:, PACK + t, :], in1=factor[t][:], op=ALU.mult)
+            copied = HALF * len([h for h in range(2) if (t, h) in on_vector])
+            if copied > 0:
+                util_copy[t] = keep.tile([P, copied], F32, name="util_copy%d" % t)
+                nc.sync.dma_start(out=util_copy[t][:], in_=util[t][:, 0:copied])
+        for t, h in on_scalar:
+            nc.scalar.activation(out=gap[:, t, columns(h)], in_=util[t][:].indirect(entries(pf_t, h)), func=ACT.Copy)
+        for t in range(PACK):
+            fused = [h for h in range(2) if (t, h) in on_vector]
+            for h in fused:
+                nc.vector.tensor_tensor(
+                    out=gap[:, t, columns(h)],
+                    in0=util[t][:].indirect(entries(pf_t, h)),
+                    in1=util_copy[t][:, columns(h)],
+                    op=ALU.subtract,
+                )
+            if len(fused) < 2:
+                fetched = slice(HALF * len(fused), S)
+                nc.vector.tensor_tensor(out=gap[:, t, fetched], in0=gap[:, t, fetched], in1=util[t][:, fetched], op=ALU.subtract)
+            nc.scalar.activation(out=gap[:, t, :], in_=gap[:, t, :], func=ACT.Tanh, scale=0.75)
 
-        def make_vict(t):
+        vict = [keep.tile([P, S // D, 1], F32, name="vict%d" % t) for t in range(PACK)]
+        for t in range(PACK):
             sets = util[t][:].rearrange("p (v d) -> p v d", d=D)
-            flat = vict[t][:].rearrange("p v o -> p (v o)")
             pair = ring.tile([P, S // D, 2], F32, name="pair")
             nc.vector.tensor_tensor(out=pair[:], in0=sets[:, :, 0:2], in1=sets[:, :, 2:4], op=ALU.min)
             nc.vector.tensor_tensor(out=vict[t][:], in0=pair[:, :, 0:1], in1=pair[:, :, 1:2], op=ALU.min)
+            flat = vict[t][:].rearrange("p v o -> p (v o)")
             nc.scalar.activation(out=flat, in_=flat, func=ACT.Copy, scale=unit_t[:, t : t + 1])
-
-        def make_marg(t):
+        marg = [keep.tile([P, S], F32, name="marg%d" % t, tag="factor%d" % t) for t in range(PACK)]
+        for t in range(PACK):
             nc.vector.scalar_tensor_tensor(
                 out=marg[t][:].rearrange("p (v d) -> p v d", d=D),
                 in0=util[t][:].rearrange("p (v d) -> p v d", d=D),
@@ -171,58 +199,35 @@ def tile_picked_ycachep_log_p_kernel(
                 op1=ALU.subtract,
             )
 
-        def make_diff(t):
-            for h in range(2):
-                cols = slice(h * HALF, (h + 1) * HALF)
-                nc.vector.tensor_tensor(
-                    out=diff[:, t, cols], in0=util[t][:].indirect(entries(pf_t, h)), in1=util_b[t][:, cols], op=ALU.subtract
-                )
-
-        def fetch_on_scalar(t):
-            for h in range(2):
-                cols = slice(h * HALF, (h + 1) * HALF)
-                nc.scalar.activation(out=diff[:, t, cols], in_=util[t][:].indirect(entries(pf_t, h)), func=ACT.Copy)
-
-        def make_tanh(t):
-            nc.scalar.activation(out=diff[:, t, :], in_=diff[:, t, :], func=ACT.Tanh, scale=0.75)
-
-        last = PACK - 1
-        for t in range(PACK):
-            make_util(t)
-        make_diff(0)
-        make_tanh(0)
-        fetch_on_scalar(last)
-        for t in range(1, last):
-            make_diff(t)
-            make_tanh(t)
-        nc.vector.tensor_tensor(out=diff[:, last, :], in0=diff[:, last, :], in1=util[last][:], op=ALU.subtract)
-        make_tanh(last)
-        for t in range(PACK):
-            make_vict(t)
-        for t in range(PACK):
-            make_marg(t)
-
         out_rows = out.rearrange("(b p) j -> p b j", p=P)
         for c, wide in enumerate(OUT_BLOCKS):
             first = sum(OUT_BLOCKS[:c])
             cols = slice(first, first + wide)
-            ladm = ring.tile([P, PACK, wide], F32, name="ladm", bufs=5)
-            nc.scalar.activation(out=ladm[:], in_=diff[:, :, cols], func=ACT.Ln, scale=0.5, bias=0.6)
+            log_adm = ring.tile([P, PACK, wide], F32, name="log_adm", bufs=len(OUT_BLOCKS))
+            nc.scalar.activation(out=log_adm[:], in_=gap[:, :, cols], func=ACT.Ln, scale=0.5, bias=0.6)
+
             hid = ring.tile([P, PACK, wide], BF16, name="hid", bufs=3, align_bytes=64)
             for t in range(PACK):
                 nc.vector.scalar_tensor_tensor(
-                    out=hid[:, t, :], in0=ladm[:, t, :], scalar=cu[:, t : t + 1], in1=marg[t][:, cols], op0=ALU.mult, op1=ALU.add
+                    out=hid[:, t, :],
+                    in0=log_adm[:, t, :],
+                    scalar=log_weight[:, t : t + 1],
+                    in1=marg[t][:, cols],
+                    op0=ALU.mult,
+                    op1=ALU.add,
                 )
+
             woven = ring.tile([P, wide, PACK], BF16, name="woven", bufs=3, align_bytes=64)
-            weave = nc.scalar.copy if c < 2 else nc.vector.tensor_copy
-            weave(out=woven[:].rearrange("p (c i) t -> p c t i", i=4), in_=hid[:].rearrange("p t (c i) -> p c t i", i=4))
+            weave = nc.scalar.copy if c < SCALAR_WEAVES else nc.vector.tensor_copy
+            weave(out=woven[:].rearrange("p (g i) t -> p g t i", i=4), in_=hid[:].rearrange("p t (g i) -> p g t i", i=4))
             h_codes = ring.tile([P, wide], U32, name="h_codes", bufs=3, align_bytes=64)
             h_plane = ring.tile([P, wide], U8, name="h_plane", bufs=3, align_bytes=64)
             nc.vector.quantize_mx(out=h_codes[:].bitcast(FP8X4), scales=h_plane[:], in_=woven[:].rearrange("p j t -> p (j t)"))
-            acc = psum.tile([P, HALF], F32, name="acc", tag="bank")
+
+            policy = psum.tile([P, HALF], F32, name="policy", tag="bank")
             for b in range(N // P):
                 nc.tensor.matmul_mx(
-                    out=acc[:, b * wide : (b + 1) * wide],
+                    out=policy[:, b * wide : (b + 1) * wide],
                     lhsT=w3_codes[:, 2 * P * b : 2 * P * (b + 1)].bitcast(FP4X4),
                     lhsT_scale=w3_plane[:, P * b : P * (b + 1)],
                     rhs=h_codes[:].bitcast(FP8X4),
@@ -230,6 +235,6 @@ def tile_picked_ycachep_log_p_kernel(
                     start=True,
                     stop=True,
                 )
-            res = ring.tile([P, N // P, wide], F32, name="res", bufs=5)
-            nc.scalar.copy(out=res[:].rearrange("p b j -> p (b j)"), in_=acc[:, 0 : 2 * wide])
-            nc.sync.dma_start(out=out_rows[:, :, cols], in_=res[:])
+            result = ring.tile([P, N // P, wide], F32, name="result", bufs=len(OUT_BLOCKS))
+            nc.scalar.copy(out=result[:].rearrange("p b j -> p (b j)"), in_=policy[:, 0 : (N // P) * wide])
+            nc.sync.dma_start(out=out_rows[:, :, cols], in_=result[:])

@@ -25,7 +25,7 @@ LINEAR_FROM = 41.0
 
 OUT_BLOCKS = (256, 256, 256, 128, 128)
 
-SCALAR_FETCHES = 3
+SCALAR_FETCHES = 4
 SCALAR_WEAVES = 2
 
 
@@ -68,8 +68,8 @@ def tile_picked_ycachep_log_p_kernel(
         nc.sync.dma_start(out=x_table[:, 0 : T // 2], in_=x_rows[:, 0 : T // 2])
         load_scale_rows(x_plane, x_scales)
         nc.sync.dma_start(out=x_table[:, T // 2 : T], in_=x_rows[:, T // 2 : T])
-        nc.sync.dma_start(pf_t[:], pf)
         load_scale_rows(w1_raw_plane, w1_scales)
+        nc.sync.dma_start(pf_t[:], pf)
 
         w_codes = [keep.tile([P, PACK, 2 * P], U8, name="w_codes%d" % side, align_bytes=64) for side in (RECY, FREQ)]
         w_plane = [keep.tile([P, PACK, P], U8, name="w_plane%d" % side, align_bytes=64) for side in (RECY, FREQ)]
@@ -183,10 +183,8 @@ def tile_picked_ycachep_log_p_kernel(
         vict = [keep.tile([P, S // D, 1], F32, name="vict%d" % t) for t in range(PACK)]
         for t in range(PACK):
             sets = util[t][:].rearrange("p (v d) -> p v d", d=D)
-            pair = ring.tile([P, S // D, 2], F32, name="pair")
-            nc.vector.tensor_tensor(out=pair[:], in0=sets[:, :, 0:2], in1=sets[:, :, 2:4], op=ALU.min)
-            nc.vector.tensor_tensor(out=vict[t][:], in0=pair[:, :, 0:1], in1=pair[:, :, 1:2], op=ALU.min)
             flat = vict[t][:].rearrange("p v o -> p (v o)")
+            nc.vector.tensor_reduce(out=flat, in_=sets, axis=mybir.AxisListType.X, op=ALU.min)
             nc.scalar.activation(out=flat, in_=flat, func=ACT.Copy, scale=unit_t[:, t : t + 1])
         marg = [keep.tile([P, S], F32, name="marg%d" % t, tag="factor%d" % t) for t in range(PACK)]
         for t in range(PACK):

from contextlib import ExitStack

import concourse.mybir as mybir

K, T, S, D, N, H = 512, 4096, 1024, 4, 256, 512
FLOPS = 2 * K * H * S * 2 + 2 * H * N * S

F32 = mybir.dt.float32
BF16 = mybir.dt.bfloat16
I32 = mybir.dt.int32
U32 = mybir.dt.uint32
U16 = mybir.dt.uint16
U8 = mybir.dt.uint8
FP8X4 = mybir.dt.float8_e4m3fn_x4
FP4X4 = mybir.dt.float4_e2m1fn_x4
ACT = mybir.ActivationFunctionType
ALU = mybir.AluOpType

P = 128
PACK = 4
HALF = S // 2
RECY, FREQ = 0, 1

LINEAR_FROM = 41.0

OUT_BLOCKS = (256, 256, 256, 128, 128)

SCALAR_FETCHES = 4
SCALAR_WEAVES = 2


def tile_picked_ycachep_log_p_kernel(
    tc, x_words, x_scales, w1_words, w1_scales, w2_words, w2_scales, unit, w3_words, w3_scales, offs, pf, out
):
    nc = tc.nc
    with ExitStack() as ctx:
        lists = ctx.enter_context(tc.tile_pool(name="lists", bufs=1))
        keep = ctx.enter_context(tc.tile_pool(name="keep", bufs=1))
        ring = ctx.enter_context(tc.tile_pool(name="ring", bufs=2))
        turns = ctx.enter_context(tc.tile_pool(name="turns", bufs=1))
        psum = ctx.enter_context(tc.psum_pool(name="psum", bufs=8))

        def load_scale_rows(plane, rows):
            for q in range(4):
                nc.sync.dma_start(out=plane[32 * q : 32 * q + 4, :].bitcast(I32), in_=rows[0, 4 * q : 4 * q + 4, :].bitcast(I32))

        def columns(h):
            return slice(h * HALF, (h + 1) * HALF)

        def entries(list_tile, h):
            return list_tile[:, h * HALF // 16 : (h + 1) * HALF // 16]

        offs_t = lists.tile([P, S // 16], U16, name="offs_t")
        pf_t = lists.tile([P, S // 16], U16, name="pf_t")
        x_table = keep.tile([P, T], I32, name="x_table", tag="table", align_bytes=64)
        x_plane = turns.tile([P, T], U8, name="x_plane", align_bytes=64, offset=0)
        w1_raw = keep.tile([P, 3 * H], U8, name="w1_raw", tag="w1_raw", align_bytes=64)
        w1_raw_words = w1_raw[:, 0 : 2 * H]
        w1_raw_plane = w1_raw[:, 2 * H : 3 * H]

        nc.vector.memset(x_plane[:, 0 : T // 2].bitcast(I32), 0)
        nc.gpsimd.memset(x_plane[:, T // 2 : T].bitcast(I32), 0)
        nc.vector.memset(w1_raw_plane.bitcast(I32), 0)

        nc.sync.dma_start(offs_t[:], offs)
        nc.scalar.dma_start(out=w1_raw_words.bitcast(I32), in_=w1_words[0].bitcast(I32))
        x_rows = x_words[0].rearrange("p n t -> p (n t)").bitcast(I32)
        nc.sync.dma_start(out=x_table[:, 0 : T // 2], in_=x_rows[:, 0 : T // 2])
        load_scale_rows(x_plane, x_scales)
        nc.sync.dma_start(out=x_table[:, T // 2 : T], in_=x_rows[:, T // 2 : T])
        load_scale_rows(w1_raw_plane, w1_scales)
        nc.sync.dma_start(pf_t[:], pf)

        w_codes = [keep.tile([P, PACK, 2 * P], U8, name="w_codes%d" % side, align_bytes=64) for side in (RECY, FREQ)]
        w_plane = [keep.tile([P, PACK, P], U8, name="w_plane%d" % side, align_bytes=64) for side in (RECY, FREQ)]

        def deal(side, raw_words, raw_plane):
            nc.vector.tensor_copy(
                out=w_codes[side][:].rearrange("p t (m b) -> p t m b", b=2),
                in_=raw_words.rearrange("p (m t b) -> p t m b", t=PACK, b=2),
            )
            nc.vector.tensor_copy(out=w_plane[side][:], in_=raw_plane.rearrange("p (m t) -> p t m", t=PACK))

        xg_plane = [keep.tile([P, HALF], U8, name="xg_plane%d" % h, align_bytes=64) for h in range(2)]
        deal(RECY, w1_raw_words, w1_raw_plane)
        for h in range(2):
            nc.vector.tensor_copy(xg_plane[h][:], x_plane[:].indirect(entries(offs_t, h)))

        xg_words = [
            turns.tile([P, HALF], U32, name="xg_words0", align_bytes=64, offset=0),
            keep.tile([P, HALF], U32, name="xg_words1", tag="w1_raw", align_bytes=64),
        ]
        late_plane = turns.tile([P, H], U8, name="late_plane", align_bytes=64, offset=4 * HALF)
        w2_raw_words = turns.tile([P, 2 * H], U8, name="w2_raw_words", align_bytes=64, offset=4 * HALF + H)
        nc.sync.dma_start(out=w2_raw_words[:].bitcast(I32), in_=w2_words[0].bitcast(I32))
        nc.gpsimd.memset(late_plane[:].bitcast(I32), 0)
        load_scale_rows(late_plane, w2_scales)
        for h in range(2):
            nc.vector.tensor_copy(xg_words[h][:], x_table[:].bitcast(U32).indirect(entries(offs_t, h)))
        deal(FREQ, w2_raw_words[:], late_plane[:])

        w3_plane = late_plane[:, 0:N]
        load_scale_rows(w3_plane, w3_scales)
        unit_t = keep.tile([P, PACK], F32, name="unit_t", tag="table", align_bytes=64)
        nc.sync.dma_start(out=unit_t[:], in_=unit.rearrange("(p t) o -> p (t o)", t=PACK))

        expo = keep.tile([P, 2 * PACK, S], F32, name="expo")
        soft = keep.tile([P, 2 * PACK, S], F32, name="soft")
        freq_banks = {}
        for side in (RECY, FREQ):
            for h in range(2):
                for t in range(PACK):
                    product = psum.tile([P, HALF], F32, name="product", tag="bank")
                    nc.tensor.matmul_mx(
                        out=product[:],
                        lhsT=w_codes[side][:, t, :].bitcast(FP4X4),
                        lhsT_scale=w_plane[side][:, t, :],
                        rhs=xg_words[h][:].bitcast(FP8X4),
                        rhs_scale=xg_plane[h][:],
                        start=True,
                        stop=True,
                    )
                    nc.scalar.activation(out=expo[:, PACK * side + t, columns(h)], in_=product[:], func=ACT.Exp)
                    if side == RECY:
                        nc.vector.tensor_copy(out=soft[:, t, columns(h)], in_=product[:])
                    else:
                        freq_banks[t, h] = product

        w3_codes = turns.tile([P, 2 * N], U8, name="w3_codes", align_bytes=64, offset=0)
        nc.sync.dma_start(out=w3_codes[:].bitcast(I32), in_=w3_words[0].bitcast(I32))
        log_weight = keep.tile([P, PACK], F32, name="log_weight")
        nc.vector.tensor_scalar(out=log_weight[:], in0=unit_t[:], scalar1=-0.4, scalar2=None, op0=ALU.mult)

        def bounded(row, cols, product):
            nc.vector.scalar_tensor_tensor(
                out=soft[:, row, cols], in0=expo[:, row, cols], scalar=LINEAR_FROM, in1=product, op0=ALU.min, op1=ALU.max
            )

        for t in range(PACK):
            nc.scalar.activation(out=expo[:, t, :], in_=expo[:, t, :], func=ACT.Ln, bias=1.0)
            bounded(t, slice(0, S), soft[:, t, :])
        for t in range(PACK):
            nc.scalar.activation(out=expo[:, PACK + t, :], in_=expo[:, PACK + t, :], func=ACT.Ln, bias=1.0)
            for h in range(2):
                bounded(PACK + t, columns(h), freq_banks[t, h][:])

        factor = [keep.tile([P, S], F32, name="factor%d" % t, tag="factor%d" % t) for t in range(PACK)]
        util = [keep.tile([P, S], F32, name="util%d" % t) for t in range(PACK)]
        for h in range(2):
            cols = columns(h)
            nc.scalar.activation(out=factor[0][:, cols], in_=soft[:, 0, cols], func=ACT.Abs_reciprocal_sqrt, bias=0.4)
            nc.vector.tensor_tensor(out=soft[:, PACK, cols], in0=soft[:, PACK, cols], in1=factor[0][:, cols], op=ALU.mult)
        for t in range(1, PACK):
            nc.scalar.activation(out=factor[t][:], in_=soft[:, t, :], func=ACT.Abs_reciprocal_sqrt, bias=0.4)
            nc.scalar.activation(out=factor[t][:], in_=factor[t][:], func=ACT.Square)

        halves = [(t, h) for t in range(PACK) for h in range(2)]
        on_vector, on_scalar = halves[:-SCALAR_FETCHES], halves[-SCALAR_FETCHES:]
        gap = keep.tile([P, PACK, S], F32, name="gap")
        util_copy = {}
        for t in range(PACK):
            nc.vector.tensor_tensor(out=util[t][:], in0=soft[:, PACK + t, :], in1=factor[t][:], op=ALU.mult)
            copied = HALF * len([h for h in range(2) if (t, h) in on_vector])
            if copied > 0:
                util_copy[t] = keep.tile([P, copied], F32, name="util_copy%d" % t)
                nc.sync.dma_start(out=util_copy[t][:], in_=util[t][:, 0:copied])
        for t, h in on_scalar:
            nc.scalar.activation(out=gap[:, t, columns(h)], in_=util[t][:].indirect(entries(pf_t, h)), func=ACT.Copy)
        for t in range(PACK):
            fused = [h for h in range(2) if (t, h) in on_vector]
            for h in fused:
                nc.vector.tensor_tensor(
                    out=gap[:, t, columns(h)],
                    in0=util[t][:].indirect(entries(pf_t, h)),
                    in1=util_copy[t][:, columns(h)],
                    op=ALU.subtract,
                )
            if len(fused) < 2:
                fetched = slice(HALF * len(fused), S)
                nc.vector.tensor_tensor(out=gap[:, t, fetched], in0=gap[:, t, fetched], in1=util[t][:, fetched], op=ALU.subtract)
            nc.scalar.activation(out=gap[:, t, :], in_=gap[:, t, :], func=ACT.Tanh, scale=0.75)

        vict = [keep.tile([P, S // D, 1], F32, name="vict%d" % t) for t in range(PACK)]
        for t in range(PACK):
            sets = util[t][:].rearrange("p (v d) -> p v d", d=D)
            flat = vict[t][:].rearrange("p v o -> p (v o)")
            nc.vector.tensor_reduce(out=flat, in_=sets, axis=mybir.AxisListType.X, op=ALU.min)
            nc.scalar.activation(out=flat, in_=flat, func=ACT.Copy, scale=unit_t[:, t : t + 1])
        marg = [keep.tile([P, S], F32, name="marg%d" % t, tag="factor%d" % t) for t in range(PACK)]
        for t in range(PACK):
            nc.vector.scalar_tensor_tensor(
                out=marg[t][:].rearrange("p (v d) -> p v d", d=D),
                in0=util[t][:].rearrange("p (v d) -> p v d", d=D),
                scalar=unit_t[:, t : t + 1],
                in1=vict[t][:].to_broadcast([P, S // D, D]),
                op0=ALU.mult,
                op1=ALU.subtract,
            )

        out_rows = out.rearrange("(b p) j -> p b j", p=P)
        for c, wide in enumerate(OUT_BLOCKS):
            first = sum(OUT_BLOCKS[:c])
            cols = slice(first, first + wide)
            log_adm = ring.tile([P, PACK, wide], F32, name="log_adm", bufs=len(OUT_BLOCKS))
            nc.scalar.activation(out=log_adm[:], in_=gap[:, :, cols], func=ACT.Ln, scale=0.5, bias=0.6)

            hid = ring.tile([P, PACK, wide], BF16, name="hid", bufs=3, align_bytes=64)
            for t in range(PACK):
                nc.vector.scalar_tensor_tensor(
                    out=hid[:, t, :],
                    in0=log_adm[:, t, :],
                    scalar=log_weight[:, t : t + 1],
                    in1=marg[t][:, cols],
                    op0=ALU.mult,
                    op1=ALU.add,
                )

            woven = ring.tile([P, wide, PACK], BF16, name="woven", bufs=3, align_bytes=64)
            weave = nc.scalar.copy if c < SCALAR_WEAVES else nc.vector.tensor_copy
            weave(out=woven[:].rearrange("p (g i) t -> p g t i", i=4), in_=hid[:].rearrange("p t (g i) -> p g t i", i=4))
            h_codes = ring.tile([P, wide], U32, name="h_codes", bufs=3, align_bytes=64)
            h_plane = ring.tile([P, wide], U8, name="h_plane", bufs=3, align_bytes=64)
            nc.vector.quantize_mx(out=h_codes[:].bitcast(FP8X4), scales=h_plane[:], in_=woven[:].rearrange("p j t -> p (j t)"))

            policy = psum.tile([P, HALF], F32, name="policy", tag="bank")
            for b in range(N // P):
                nc.tensor.matmul_mx(
                    out=policy[:, b * wide : (b + 1) * wide],
                    lhsT=w3_codes[:, 2 * P * b : 2 * P * (b + 1)].bitcast(FP4X4),
                    lhsT_scale=w3_plane[:, P * b : P * (b + 1)],
                    rhs=h_codes[:].bitcast(FP8X4),
                    rhs_scale=h_plane[:],
                    start=True,
                    stop=True,
                )
            result = ring.tile([P, N // P, wide], F32, name="result", bufs=len(OUT_BLOCKS))
            nc.scalar.copy(out=result[:].rearrange("p b j -> p (b j)"), in_=policy[:, 0 : (N // P) * wide])
            nc.sync.dma_start(out=out_rows[:, :, cols], in_=result[:])
